import numpy as np, ml_dtypes
CORES = [83,85,87,115,117,119]
N = 6
import mx_ref
NC, G = 128, 4
C = np.float32(0.029)
BF = ml_dtypes.bfloat16
def cut(t, i, w=512):
    return t[:, w * i:w * i + w]
def tile(rs):
    return np.stack(rs, axis=2).reshape(128, -1).astype(BF)
def layer(w, X):
    out = []
    for i in range(G):
        for t in range(len(X)):
            p = mx_ref.matmul(mx_ref.quantize(cut(w, len(X) * i + t)), X[t])
            z = p if t == 0 else z + p
        out.append(z)
    return out
def act(Z):
    return [np.maximum(z, 0) * C for z in Z]
def setup_inputs(rng):
    def f(*shape):
        return mx_ref.flush((rng.standard_normal(shape, dtype=np.float32) * np.exp2(rng.integers(-2, 3, shape[:-1] + (1,)))).astype(BF))
    return {"x": f(N, 128, 4 * NC), "w1": f(N, 128, G * 512), "w2": f(N, 128, 512)}
def setup_inputs_blocks(rng):
    d = setup_inputs(rng)
    for k in ("x", "w1", "w2"): d[k] = mx_ref.spread(d[k], rng, 2)
    return d
def setup_inputs_wide(rng):
    d = setup_inputs(rng)
    for k in ("x", "w1", "w2"): d[k] = mx_ref.flush((d[k].astype(np.float32) * np.exp2(rng.integers(-6, 7, (N, 1, 1))).astype(np.float32)).astype(BF))
    return d
def reference(x, w1, w2):
    X = [mx_ref.quantize(x[j]) for j in range(N)]
    y = np.zeros((N, 128, NC), np.float32)
    for c in range(N):
        for r in range(N):
            p = mx_ref.matmul(mx_ref.quantize(w2[r]), mx_ref.quantize(tile(act(layer(w1[r], [X[c]])))))
            y[c] = p if r == 0 else y[c] + p
    return {"y": y}

@@ -1,0 +1,145 @@
+from concourse.bass import DstId, RemoteDMATransfer
+from concourse.mybir import dt, AluOpType, ActivationFunctionType
+
+W = 128
+NS = 6
+CH = 0.029
+ON_SLOT = {1: 1, 2: 3}
+OFF_SLOT = {0: 2, 1: 4, 2: 5}
+STAGES = (((1,), (0,)), ((2,), (1,)), ((), (2,)))
+
+SCRATCH = {
+    "xb": ("sbuf", [128, 4 * W], "bfloat16"),
+    "w1b": ("sbuf", [128, 16 * W], "bfloat16"),
+    "w2b": ("sbuf", [128, 4 * W], "bfloat16"),
+    "xq": ("sbuf", [128, NS * W], "float8_e4m3fn_x4"),
+    "xs": ("sbuf", [128, NS * W], "uint8"),
+    "w1q": ("sbuf", [128, 4 * W], "float8_e4m3fn_x4"),
+    "w1s": ("sbuf", [128, 4 * W], "uint8"),
+    "w2q": ("sbuf", [128, W], "float8_e4m3fn_x4"),
+    "w2s": ("sbuf", [128, W], "uint8"),
+    "h": ("sbuf", [128, NS * 4 * W], "bfloat16"),
+    "hq": ("sbuf", [128, NS * W], "float8_e4m3fn_x4"),
+    "hs": ("sbuf", [128, NS * W], "uint8"),
+    "yp": ("sbuf", [128, NS * W], "float32"),
+    "yl": ("sbuf", [128, NS * W], "float32"),
+    "acc": ("sbuf", [128, W], "float32"),
+    "ps": ("psum", [128, 512 * 8], "float32"),
+}
+SEMAPHORES = (["lx", "lw1a", "lw1b", "lw2", "qx", "qw1a", "qw1b", "qw2", "sent", "stored"]
+              + ["mm%d_%d" % (s, b) for s in range(NS) for b in range(4)]
+              + ["%s%d" % (k, s) for k in ("rl", "qh", "m2", "cp") for s in range(NS)]
+              + ["%s%d" % (k, s) for k in ("xa", "ya", "ad") for s in range(1, NS)])
+
+
+def rank_program(g, core, T, topo):
+    if T.rank_of(core) is None:
+        return
+    sem = T.sem
+    here = [c for c in T.cores if topo.chip(c) == topo.chip(core)]
+    away = [c for c in T.cores if topo.chip(c) != topo.chip(core)]
+    p, n = here.index(core), len(here)
+
+    off_mask = topo.mask(core, away[0])
+    on_mask = topo.mask(core, here[(p + 1) % n]) & ~off_mask
+    engines = {True: bin(on_mask).count("1"), False: bin(off_mask).count("1")}
+    sent = [0]
+
+    def cols(s, w=W):
+        return slice(w * s, w * s + w)
+
+    def transfer(src, dst, to, on_chip, remote_sem):
+        rid, pid, _ = topo.addr(to)
+        sent[0] += engines[on_chip]
+        return RemoteDMATransfer(dst_ids=[DstId(rid=rid, pnc=pid)], dma_engine_mask=on_mask if on_chip else off_mask,
+                                 remote_sem=remote_sem, src=src, dst=dst)
+
+    half = 8 * W
+    g.sync.dma_start(T.xb[:], T.x[:]).then_inc(sem.lx, 16)
+    g.sync.dma_start(T.w1b[:, 0:half], T.w1[:, 0:half]).then_inc(sem.lw1a, 16)
+    g.sync.dma_start(T.w1b[:, half:2 * half], T.w1[:, half:2 * half]).then_inc(sem.lw1b, 16)
+    g.sync.dma_start(T.w2b[:], T.w2[:]).then_inc(sem.lw2, 16)
+
+    g.vector.wait_ge(sem.lx, 16)
+    g.vector.quantize_mx(T.xq[:, cols(0)], T.xs[:, cols(0)], T.xb[:]).then_inc(sem.qx, 1)
+    g.vector.wait_ge(sem.lw1a, 16)
+    g.vector.quantize_mx(T.w1q[:, 0:2 * W], T.w1s[:, 0:2 * W], T.w1b[:, 0:half]).then_inc(sem.qw1a, 1)
+    g.vector.wait_ge(sem.lw1b, 16)
+    g.vector.quantize_mx(T.w1q[:, 2 * W:4 * W], T.w1s[:, 2 * W:4 * W], T.w1b[:, half:2 * half]).then_inc(sem.qw1b, 1)
+
+    g.wait_ge(sem.qx, 1)
+    for ons, offs in STAGES:
+        dests = [(away[(p + d) % n], False, OFF_SLOT[d]) for d in offs] + [(here[(p + d) % n], True, ON_SLOT[d]) for d in ons]
+        g.remote_dma_fused([transfer(T.xq[:, cols(0)].bitcast(dt.uint8), T.xq[:, cols(s)].bitcast(dt.uint8), to, oc, sem["xa%d" % s])
+                            for to, oc, s in dests], local_sem=sem.sent)
+        g.remote_dma_fused([transfer(T.xs[:, cols(0)], T.xs[:, cols(s)], to, oc, sem["xa%d" % s])
+                            for to, oc, s in dests], local_sem=sem.sent)
+
+    owner = {ON_SLOT[d]: (here[(p - d) % n], True) for d in ON_SLOT}
+    owner.update({OFF_SLOT[d]: (away[(p - d) % n], False) for d in OFF_SLOT})
+    order = (1, 2, 3, 0)
+
+    def bank(s, b):
+        k = 512 * (4 * (s % 2) + b)
+        return T.ps[:, k:k + W]
+
+    def layer1(s):
+        if s == 0:
+            g.tensor.wait_ge(sem.qx, 1)
+            g.tensor.wait_ge(sem.qw1a, 1)
+        else:
+            g.tensor.wait_ge(sem["xa%d" % s], 2 * engines[owner[s][1]])
+        for b in order:
+            if s == 0 and b == 2:
+                g.tensor.wait_ge(sem.qw1b, 1)
+            if s >= 2 and b == 0:
+                g.tensor.wait_ge(sem["cp%d" % (s - 2)], 1)
+            g.tensor.matmul_mx(bank(s, b), T.w1q[:, cols(b)], T.w1s[:, cols(b)], T.xq[:, cols(s)], T.xs[:, cols(s)],
+                               True, True).then_inc(sem["mm%d_%d" % (s, b)], 1)
+        for i, b in enumerate(order):
+            out = T.h[:, 4 * W * s + b:4 * W * (s + 1):4]
+            if i % 2 == 0:
+                g.scalar.wait_ge(sem["mm%d_%d" % (s, b)], 1)
+                g.scalar.activation(out, bank(s, b), ActivationFunctionType.Relu, scale=CH).then_inc(sem["rl%d" % s], 1)
+            else:
+                g.vector.wait_ge(sem["mm%d_%d" % (s, b)], 1)
+                g.vector.tensor_scalar(out, bank(s, b), 0.0, CH, AluOpType.max, AluOpType.mult).then_inc(sem["rl%d" % s], 1)
+        if s == 0:
+            g.vector.wait_ge(sem.lw2, 16)
+            g.vector.quantize_mx(T.w2q[:], T.w2s[:], T.w2b[:]).then_inc(sem.qw2, 1)
+        g.vector.wait_ge(sem["rl%d" % s], 4)
+        g.vector.quantize_mx(T.hq[:, cols(s)], T.hs[:, cols(s)], T.h[:, cols(s, 4 * W)]).then_inc(sem["qh%d" % s], 1)
+
+    def layer2(s):
+        if s == 0:
+            g.tensor.wait_ge(sem.qw2, 1)
+        g.tensor.wait_ge(sem["qh%d" % s], 1)
+        g.tensor.matmul_mx(bank(s, 0), T.w2q[:], T.w2s[:], T.hq[:, cols(s)], T.hs[:, cols(s)], True, True).then_inc(sem["m2%d" % s], 1)
+        g.scalar.wait_ge(sem["m2%d" % s], 1)
+        g.scalar.activation(T.yp[:, cols(s)], bank(s, 0), ActivationFunctionType.Copy).then_inc(sem["cp%d" % s], 1)
+
+    layer1(0)
+    layer2(0)
+    for ons, offs in STAGES:
+        slots = [ON_SLOT[d] for d in ons] + [OFF_SLOT[d] for d in offs]
+        for s in slots:
+            layer1(s)
+        for s in slots:
+            layer2(s)
+        for s in slots:
+            g.wait_ge(sem["cp%d" % s], 1)
+        g.remote_dma_fused([transfer(T.yp[:, cols(s)], T.yl[:, cols(s)], owner[s][0], owner[s][1], sem["ya%d" % s])
+                            for s in reversed(slots)], local_sem=sem.sent)
+
+    g.vector.wait_ge(sem.cp0, 1)
+    prev = T.yp[:, cols(0)]
+    for s in range(1, NS):
+        if s > 1:
+            g.vector.wait_ge(sem["ad%d" % (s - 1)], 1)
+        g.vector.wait_ge(sem["ya%d" % s], engines[owner[s][1]])
+        g.vector.tensor_tensor(T.acc[:], prev, T.yl[:, cols(s)], AluOpType.add).then_inc(sem["ad%d" % s], 1)
+        prev = T.acc[:]
+    g.sync.wait_ge(sem["ad%d" % (NS - 1)], 1)
+    g.sync.dma_start(T.y[:], T.acc[:]).then_inc(sem.stored, 16)
+    g.sync.wait_ge(sem.stored, 16)
+    g.wait_ge(sem.sent, sent[0])

@@ -4,9 +4,13 @@ from concourse.mybir import dt, AluOpType, ActivationFunctionType
 W = 128
 NS = 6
 CH = 0.029
-ON_SLOT = {1: 1, 2: 3}
-OFF_SLOT = {0: 2, 1: 4, 2: 5}
-STAGES = (((1,), (0,)), ((2,), (1,)), ((), (2,)))
+NZ, NY = 6, 2
+ON1, ON2, OFF0, OFF1, OFF2 = ("on", 1), ("on", 2), ("off", 0), ("off", 1), ("off", 2)
+ORDER = (OFF0, ON1, OFF1, ON2, OFF2)
+SENDS = (("codes", (OFF0,)), ("planes", (ON1, OFF0)), ("codes", (ON1, OFF1)),
+         ("planes", (ON2, OFF1, OFF2)), ("codes", (ON2,)))
+RELAYED = OFF2
+SLICES = ((OFF0,), (ON1, OFF1), (ON2,), (OFF2,))
 
 SCRATCH = {
     "xb": ("sbuf", [128, 4 * W], "bfloat16"),
@@ -24,12 +28,13 @@ SCRATCH = {
     "yp": ("sbuf", [128, NS * W], "float32"),
     "yl": ("sbuf", [128, NS * W], "float32"),
     "acc": ("sbuf", [128, W], "float32"),
-    "ps": ("psum", [128, 512 * 8], "float32"),
+    "ps": ("psum", [128, 512 * (NZ + NY)], "float32"),
 }
-SEMAPHORES = (["lx", "lw1a", "lw1b", "lw2", "qx", "qw1a", "qw1b", "qw2", "sent", "stored"]
-              + ["mm%d_%d" % (s, b) for s in range(NS) for b in range(4)]
-              + ["%s%d" % (k, s) for k in ("rl", "qh", "m2", "cp") for s in range(NS)]
-              + ["%s%d" % (k, s) for k in ("xa", "ya", "ad") for s in range(1, NS)])
+SEMAPHORES = (["lx", "lw1a", "lw1b", "lw2", "qx", "qw1a", "qw1b", "qw2", "sent", "stored", "xc"]
+              + ["%s%d_%d" % (k, s, b) for k in ("mm", "rl") for s in range(NS) for b in range(4)]
+              + ["%s%d" % (k, s) for k in ("qh", "m2", "cp") for s in range(NS)]
+              + ["xa%d" % r for r in range(NS)]
+              + ["%s%d" % (k, s) for k in ("ya", "ad") for s in range(1, NS)])
 
 
 def rank_program(g, core, T, topo):
@@ -39,20 +44,33 @@ def rank_program(g, core, T, topo):
     here = [c for c in T.cores if topo.chip(c) == topo.chip(core)]
     away = [c for c in T.cores if topo.chip(c) != topo.chip(core)]
     p, n = here.index(core), len(here)
+    slot = {k: i + 1 for i, k in enumerate(ORDER)}
+
+    def dest(k):
+        return (here if k[0] == "on" else away)[(p + k[1]) % n]
+
+    def owner(k):
+        return (here if k[0] == "on" else away)[(p - k[1]) % n]
 
     off_mask = topo.mask(core, away[0])
-    on_mask = topo.mask(core, here[(p + 1) % n]) & ~off_mask
-    engines = {True: bin(on_mask).count("1"), False: bin(off_mask).count("1")}
+    masks = {"off": off_mask, "on": topo.mask(core, here[(p + 1) % n]) & ~off_mask}
+    engines = {k: bin(m).count("1") for k, m in masks.items()}
     sent = [0]
 
     def cols(s, w=W):
         return slice(w * s, w * s + w)
 
-    def transfer(src, dst, to, on_chip, remote_sem):
-        rid, pid, _ = topo.addr(to)
-        sent[0] += engines[on_chip]
-        return RemoteDMATransfer(dst_ids=[DstId(rid=rid, pnc=pid)], dma_engine_mask=on_mask if on_chip else off_mask,
-                                 remote_sem=remote_sem, src=src, dst=dst)
+    def codes(s):
+        return T.xq[:, cols(s)].bitcast(dt.uint8)
+
+    def plane(s):
+        return T.xs[:, cols(s)]
+
+    def transfer(src, dsts, way, remote_sem):
+        sent[0] += engines[way]
+        addr = [topo.addr(to) for to, _ in dsts]
+        return RemoteDMATransfer(dst_ids=[DstId(rid=a[0], pnc=a[1]) for a in addr], dma_engine_mask=masks[way],
+                                 remote_sem=remote_sem, srcs=[src], dsts=[v for _, v in dsts])
 
     half = 8 * W
     g.sync.dma_start(T.xb[:], T.x[:]).then_inc(sem.lx, 16)
@@ -68,19 +86,35 @@ def rank_program(g, core, T, topo):
     g.vector.quantize_mx(T.w1q[:, 2 * W:4 * W], T.w1s[:, 2 * W:4 * W], T.w1b[:, half:2 * half]).then_inc(sem.qw1b, 1)
 
     g.wait_ge(sem.qx, 1)
-    for ons, offs in STAGES:
-        dests = [(away[(p + d) % n], False, OFF_SLOT[d]) for d in offs] + [(here[(p + d) % n], True, ON_SLOT[d]) for d in ons]
-        g.remote_dma_fused([transfer(T.xq[:, cols(0)].bitcast(dt.uint8), T.xq[:, cols(s)].bitcast(dt.uint8), to, oc, sem["xa%d" % s])
-                            for to, oc, s in dests], local_sem=sem.sent)
-        g.remote_dma_fused([transfer(T.xs[:, cols(0)], T.xs[:, cols(s)], to, oc, sem["xa%d" % s])
-                            for to, oc, s in dests], local_sem=sem.sent)
+    for what, kinds in SENDS:
+        view = codes if what == "codes" else plane
+        transfers = []
+        for way in ("off", "on"):
+            ks = [k for k in kinds if k[0] == way]
+            if ks:
+                rs = sem.xc if what == "codes" and ks == [OFF0] else sem["xa%d" % T.rank_of(core)]
+                transfers.append(transfer(view(0), [(dest(k), view(slot[k])) for k in ks], way, rs))
+        g.remote_dma_fused(transfers, local_sem=sem.sent)
+    g.wait_ge(sem.xc, engines["off"])
+    g.remote_dma_fused([transfer(codes(slot[OFF0]), [(here[(p + RELAYED[1]) % n], codes(slot[RELAYED]))], "on",
+                                 sem["xa%d" % T.rank_of(owner(OFF0))])], local_sem=sem.sent)
 
-    owner = {ON_SLOT[d]: (here[(p - d) % n], True) for d in ON_SLOT}
-    owner.update({OFF_SLOT[d]: (away[(p - d) % n], False) for d in OFF_SLOT})
-    order = (1, 2, 3, 0)
+    def wait_x(k):
+        xa = sem["xa%d" % T.rank_of(owner(k))]
+        if k == OFF0:
+            g.tensor.wait_ge(sem.xc, engines["off"])
+            g.tensor.wait_ge(xa, engines["off"])
+        elif k == RELAYED:
+            g.tensor.wait_ge(xa, engines["off"] + engines["on"])
+        else:
+            g.tensor.wait_ge(xa, 2 * engines[k[0]])
 
-    def bank(s, b):
-        k = 512 * (4 * (s % 2) + b)
+    def zbank(s, b):
+        k = 512 * ((4 * s + b) % NZ)
+        return T.ps[:, k:k + W]
+
+    def ybank(s):
+        k = 512 * (NZ + s % NY)
         return T.ps[:, k:k + W]
 
     def layer1(s):
@@ -88,55 +122,60 @@ def rank_program(g, core, T, topo):
             g.tensor.wait_ge(sem.qx, 1)
             g.tensor.wait_ge(sem.qw1a, 1)
         else:
-            g.tensor.wait_ge(sem["xa%d" % s], 2 * engines[owner[s][1]])
-        for b in order:
+            wait_x(ORDER[s - 1])
+        for b in range(4):
             if s == 0 and b == 2:
                 g.tensor.wait_ge(sem.qw1b, 1)
-            if s >= 2 and b == 0:
-                g.tensor.wait_ge(sem["cp%d" % (s - 2)], 1)
-            g.tensor.matmul_mx(bank(s, b), T.w1q[:, cols(b)], T.w1s[:, cols(b)], T.xq[:, cols(s)], T.xs[:, cols(s)],
+            before = 4 * s + b - NZ
+            if before >= 0:
+                g.tensor.wait_ge(sem["rl%d_%d" % (before // 4, before % 4)], 1)
+            g.tensor.matmul_mx(zbank(s, b), T.w1q[:, cols(b)], T.w1s[:, cols(b)], T.xq[:, cols(s)], T.xs[:, cols(s)],
                                True, True).then_inc(sem["mm%d_%d" % (s, b)], 1)
-        for i, b in enumerate(order):
-            out = T.h[:, 4 * W * s + b:4 * W * (s + 1):4]
-            if i % 2 == 0:
-                g.scalar.wait_ge(sem["mm%d_%d" % (s, b)], 1)
-                g.scalar.activation(out, bank(s, b), ActivationFunctionType.Relu, scale=CH).then_inc(sem["rl%d" % s], 1)
+        for b in range(4):
+            out, mm, rl = T.h[:, 4 * W * s + b:4 * W * (s + 1):4], sem["mm%d_%d" % (s, b)], sem["rl%d_%d" % (s, b)]
+            if b % 2 == 0:
+                g.scalar.wait_ge(mm, 1)
+                g.scalar.activation(out, zbank(s, b), ActivationFunctionType.Relu, scale=CH).then_inc(rl, 1)
             else:
-                g.vector.wait_ge(sem["mm%d_%d" % (s, b)], 1)
-                g.vector.tensor_scalar(out, bank(s, b), 0.0, CH, AluOpType.max, AluOpType.mult).then_inc(sem["rl%d" % s], 1)
+                g.vector.wait_ge(mm, 1)
+                g.vector.tensor_scalar(out, zbank(s, b), 0.0, CH, AluOpType.max, AluOpType.mult).then_inc(rl, 1)
         if s == 0:
             g.vector.wait_ge(sem.lw2, 16)
             g.vector.quantize_mx(T.w2q[:], T.w2s[:], T.w2b[:]).then_inc(sem.qw2, 1)
-        g.vector.wait_ge(sem["rl%d" % s], 4)
+        for b in range(4):
+            g.vector.wait_ge(sem["rl%d_%d" % (s, b)], 1)
         g.vector.quantize_mx(T.hq[:, cols(s)], T.hs[:, cols(s)], T.h[:, cols(s, 4 * W)]).then_inc(sem["qh%d" % s], 1)
 
     def layer2(s):
         if s == 0:
             g.tensor.wait_ge(sem.qw2, 1)
         g.tensor.wait_ge(sem["qh%d" % s], 1)
-        g.tensor.matmul_mx(bank(s, 0), T.w2q[:], T.w2s[:], T.hq[:, cols(s)], T.hs[:, cols(s)], True, True).then_inc(sem["m2%d" % s], 1)
+        if s >= NY:
+            g.tensor.wait_ge(sem["cp%d" % (s - NY)], 1)
+        g.tensor.matmul_mx(ybank(s), T.w2q[:], T.w2s[:], T.hq[:, cols(s)], T.hs[:, cols(s)], True, True).then_inc(sem["m2%d" % s], 1)
         g.scalar.wait_ge(sem["m2%d" % s], 1)
-        g.scalar.activation(T.yp[:, cols(s)], bank(s, 0), ActivationFunctionType.Copy).then_inc(sem["cp%d" % s], 1)
+        g.scalar.activation(T.yp[:, cols(s)], ybank(s), ActivationFunctionType.Copy).then_inc(sem["cp%d" % s], 1)
 
     layer1(0)
     layer2(0)
-    for ons, offs in STAGES:
-        slots = [ON_SLOT[d] for d in ons] + [OFF_SLOT[d] for d in offs]
-        for s in slots:
-            layer1(s)
-        for s in slots:
-            layer2(s)
-        for s in slots:
-            g.wait_ge(sem["cp%d" % s], 1)
-        g.remote_dma_fused([transfer(T.yp[:, cols(s)], T.yl[:, cols(s)], owner[s][0], owner[s][1], sem["ya%d" % s])
-                            for s in reversed(slots)], local_sem=sem.sent)
+    layer1(1)
+    for s in range(1, NS):
+        if s + 1 < NS:
+            layer1(s + 1)
+        layer2(s)
+
+    for kinds in SLICES:
+        for k in kinds:
+            g.wait_ge(sem["cp%d" % slot[k]], 1)
+        g.remote_dma_fused([transfer(T.yp[:, cols(slot[k])], [(owner(k), T.yl[:, cols(slot[k])])], k[0], sem["ya%d" % slot[k]])
+                            for k in kinds], local_sem=sem.sent)
 
     g.vector.wait_ge(sem.cp0, 1)
     prev = T.yp[:, cols(0)]
     for s in range(1, NS):
         if s > 1:
             g.vector.wait_ge(sem["ad%d" % (s - 1)], 1)
-        g.vector.wait_ge(sem["ya%d" % s], engines[owner[s][1]])
+        g.vector.wait_ge(sem["ya%d" % s], engines[ORDER[s - 1][0]])
         g.vector.tensor_tensor(T.acc[:], prev, T.yl[:, cols(s)], AluOpType.add).then_inc(sem["ad%d" % s], 1)
         prev = T.acc[:]
     g.sync.wait_ge(sem["ad%d" % (NS - 1)], 1)

from concourse.bass import DstId, RemoteDMATransfer
from concourse.mybir import dt, AluOpType, ActivationFunctionType

W = 128
NS = 6
CH = 0.029
NZ, NY = 6, 2
ON1, ON2, OFF0, OFF1, OFF2 = ("on", 1), ("on", 2), ("off", 0), ("off", 1), ("off", 2)
ORDER = (OFF0, ON1, OFF1, ON2, OFF2)
SENDS = (("codes", (OFF0,)), ("planes", (ON1, OFF0)), ("codes", (ON1, OFF1)),
         ("planes", (ON2, OFF1, OFF2)), ("codes", (ON2,)))
RELAYED = OFF2
SLICES = ((OFF0,), (ON1, OFF1), (ON2,), (OFF2,))

SCRATCH = {
    "xb": ("sbuf", [128, 4 * W], "bfloat16"),
    "w1b": ("sbuf", [128, 16 * W], "bfloat16"),
    "w2b": ("sbuf", [128, 4 * W], "bfloat16"),
    "xq": ("sbuf", [128, NS * W], "float8_e4m3fn_x4"),
    "xs": ("sbuf", [128, NS * W], "uint8"),
    "w1q": ("sbuf", [128, 4 * W], "float8_e4m3fn_x4"),
    "w1s": ("sbuf", [128, 4 * W], "uint8"),
    "w2q": ("sbuf", [128, W], "float8_e4m3fn_x4"),
    "w2s": ("sbuf", [128, W], "uint8"),
    "h": ("sbuf", [128, NS * 4 * W], "bfloat16"),
    "hq": ("sbuf", [128, NS * W], "float8_e4m3fn_x4"),
    "hs": ("sbuf", [128, NS * W], "uint8"),
    "yp": ("sbuf", [128, NS * W], "float32"),
    "yl": ("sbuf", [128, NS * W], "float32"),
    "acc": ("sbuf", [128, W], "float32"),
    "ps": ("psum", [128, 512 * (NZ + NY)], "float32"),
}
SEMAPHORES = (["lx", "lw1a", "lw1b", "lw2", "qx", "qw1a", "qw1b", "qw2", "sent", "stored", "xc"]
              + ["%s%d_%d" % (k, s, b) for k in ("mm", "rl") for s in range(NS) for b in range(4)]
              + ["%s%d" % (k, s) for k in ("qh", "m2", "cp") for s in range(NS)]
              + ["xa%d" % r for r in range(NS)]
              + ["%s%d" % (k, s) for k in ("ya", "ad") for s in range(1, NS)])


def rank_program(g, core, T, topo):
    if T.rank_of(core) is None:
        return
    sem = T.sem
    here = [c for c in T.cores if topo.chip(c) == topo.chip(core)]
    away = [c for c in T.cores if topo.chip(c) != topo.chip(core)]
    p, n = here.index(core), len(here)
    slot = {k: i + 1 for i, k in enumerate(ORDER)}

    def dest(k):
        return (here if k[0] == "on" else away)[(p + k[1]) % n]

    def owner(k):
        return (here if k[0] == "on" else away)[(p - k[1]) % n]

    off_mask = topo.mask(core, away[0])
    masks = {"off": off_mask, "on": topo.mask(core, here[(p + 1) % n]) & ~off_mask}
    engines = {k: bin(m).count("1") for k, m in masks.items()}
    sent = [0]

    def cols(s, w=W):
        return slice(w * s, w * s + w)

    def codes(s):
        return T.xq[:, cols(s)].bitcast(dt.uint8)

    def plane(s):
        return T.xs[:, cols(s)]

    def transfer(src, dsts, way, remote_sem):
        sent[0] += engines[way]
        addr = [topo.addr(to) for to, _ in dsts]
        return RemoteDMATransfer(dst_ids=[DstId(rid=a[0], pnc=a[1]) for a in addr], dma_engine_mask=masks[way],
                                 remote_sem=remote_sem, srcs=[src], dsts=[v for _, v in dsts])

    half = 8 * W
    g.sync.dma_start(T.xb[:], T.x[:]).then_inc(sem.lx, 16)
    g.sync.dma_start(T.w1b[:, 0:half], T.w1[:, 0:half]).then_inc(sem.lw1a, 16)
    g.sync.dma_start(T.w1b[:, half:2 * half], T.w1[:, half:2 * half]).then_inc(sem.lw1b, 16)
    g.sync.dma_start(T.w2b[:], T.w2[:]).then_inc(sem.lw2, 16)

    g.vector.wait_ge(sem.lx, 16)
    g.vector.quantize_mx(T.xq[:, cols(0)], T.xs[:, cols(0)], T.xb[:]).then_inc(sem.qx, 1)
    g.vector.wait_ge(sem.lw1a, 16)
    g.vector.quantize_mx(T.w1q[:, 0:2 * W], T.w1s[:, 0:2 * W], T.w1b[:, 0:half]).then_inc(sem.qw1a, 1)
    g.vector.wait_ge(sem.lw1b, 16)
    g.vector.quantize_mx(T.w1q[:, 2 * W:4 * W], T.w1s[:, 2 * W:4 * W], T.w1b[:, half:2 * half]).then_inc(sem.qw1b, 1)

    g.wait_ge(sem.qx, 1)
    for what, kinds in SENDS:
        view = codes if what == "codes" else plane
        transfers = []
        for way in ("off", "on"):
            ks = [k for k in kinds if k[0] == way]
            if ks:
                rs = sem.xc if what == "codes" and ks == [OFF0] else sem["xa%d" % T.rank_of(core)]
                transfers.append(transfer(view(0), [(dest(k), view(slot[k])) for k in ks], way, rs))
        g.remote_dma_fused(transfers, local_sem=sem.sent)
    g.wait_ge(sem.xc, engines["off"])
    g.remote_dma_fused([transfer(codes(slot[OFF0]), [(here[(p + RELAYED[1]) % n], codes(slot[RELAYED]))], "on",
                                 sem["xa%d" % T.rank_of(owner(OFF0))])], local_sem=sem.sent)

    def wait_x(k):
        xa = sem["xa%d" % T.rank_of(owner(k))]
        if k == OFF0:
            g.tensor.wait_ge(sem.xc, engines["off"])
            g.tensor.wait_ge(xa, engines["off"])
        elif k == RELAYED:
            g.tensor.wait_ge(xa, engines["off"] + engines["on"])
        else:
            g.tensor.wait_ge(xa, 2 * engines[k[0]])

    def zbank(s, b):
        k = 512 * ((4 * s + b) % NZ)
        return T.ps[:, k:k + W]

    def ybank(s):
        k = 512 * (NZ + s % NY)
        return T.ps[:, k:k + W]

    def layer1(s):
        if s == 0:
            g.tensor.wait_ge(sem.qx, 1)
            g.tensor.wait_ge(sem.qw1a, 1)
        else:
            wait_x(ORDER[s - 1])
        for b in range(4):
            if s == 0 and b == 2:
                g.tensor.wait_ge(sem.qw1b, 1)
            before = 4 * s + b - NZ
            if before >= 0:
                g.tensor.wait_ge(sem["rl%d_%d" % (before // 4, before % 4)], 1)
            g.tensor.matmul_mx(zbank(s, b), T.w1q[:, cols(b)], T.w1s[:, cols(b)], T.xq[:, cols(s)], T.xs[:, cols(s)],
                               True, True).then_inc(sem["mm%d_%d" % (s, b)], 1)
        for b in range(4):
            out, mm, rl = T.h[:, 4 * W * s + b:4 * W * (s + 1):4], sem["mm%d_%d" % (s, b)], sem["rl%d_%d" % (s, b)]
            if b % 2 == 0:
                g.scalar.wait_ge(mm, 1)
                g.scalar.activation(out, zbank(s, b), ActivationFunctionType.Relu, scale=CH).then_inc(rl, 1)
            else:
                g.vector.wait_ge(mm, 1)
                g.vector.tensor_scalar(out, zbank(s, b), 0.0, CH, AluOpType.max, AluOpType.mult).then_inc(rl, 1)
        if s == 0:
            g.vector.wait_ge(sem.lw2, 16)
            g.vector.quantize_mx(T.w2q[:], T.w2s[:], T.w2b[:]).then_inc(sem.qw2, 1)
        for b in range(4):
            g.vector.wait_ge(sem["rl%d_%d" % (s, b)], 1)
        g.vector.quantize_mx(T.hq[:, cols(s)], T.hs[:, cols(s)], T.h[:, cols(s, 4 * W)]).then_inc(sem["qh%d" % s], 1)

    def layer2(s):
        if s == 0:
            g.tensor.wait_ge(sem.qw2, 1)
        g.tensor.wait_ge(sem["qh%d" % s], 1)
        if s >= NY:
            g.tensor.wait_ge(sem["cp%d" % (s - NY)], 1)
        g.tensor.matmul_mx(ybank(s), T.w2q[:], T.w2s[:], T.hq[:, cols(s)], T.hs[:, cols(s)], True, True).then_inc(sem["m2%d" % s], 1)
        g.scalar.wait_ge(sem["m2%d" % s], 1)
        g.scalar.activation(T.yp[:, cols(s)], ybank(s), ActivationFunctionType.Copy).then_inc(sem["cp%d" % s], 1)

    layer1(0)
    layer2(0)
    layer1(1)
    for s in range(1, NS):
        if s + 1 < NS:
            layer1(s + 1)
        layer2(s)

    for kinds in SLICES:
        for k in kinds:
            g.wait_ge(sem["cp%d" % slot[k]], 1)
        g.remote_dma_fused([transfer(T.yp[:, cols(slot[k])], [(owner(k), T.yl[:, cols(slot[k])])], k[0], sem["ya%d" % slot[k]])
                            for k in kinds], local_sem=sem.sent)

    g.vector.wait_ge(sem.cp0, 1)
    prev = T.yp[:, cols(0)]
    for s in range(1, NS):
        if s > 1:
            g.vector.wait_ge(sem["ad%d" % (s - 1)], 1)
        g.vector.wait_ge(sem["ya%d" % s], engines[ORDER[s - 1][0]])
        g.vector.tensor_tensor(T.acc[:], prev, T.yl[:, cols(s)], AluOpType.add).then_inc(sem["ad%d" % s], 1)
        prev = T.acc[:]
    g.sync.wait_ge(sem["ad%d" % (NS - 1)], 1)
    g.sync.dma_start(T.y[:], T.acc[:]).then_inc(sem.stored, 16)
    g.sync.wait_ge(sem.stored, 16)
    g.wait_ge(sem.sent, sent[0])
